import numpy as np
import ml_dtypes


def mxq(x, axis, fmt="e4m3"):
    dtype, down = {"e4m3": (ml_dtypes.float8_e4m3fn, 7), "e5m2": (ml_dtypes.float8_e5m2, 14)}[fmt]
    v = np.moveaxis(np.asarray(x, np.float32).astype(ml_dtypes.bfloat16).astype(np.float64), axis, -1)
    blocks = v.reshape(v.shape[:-1] + (-1, 32))
    amax = np.abs(blocks).max(-1, keepdims=True)
    byte = np.maximum(np.where(amax > 0, np.frexp(amax)[1] - 1 + 127, 0) - down, 1)
    scale = np.exp2(byte - 127.0)
    codes = (blocks / scale).astype(np.float32).astype(dtype).astype(np.float64)
    return np.moveaxis((codes * scale).reshape(v.shape), -1, axis)


WIDE = False


def mx_kscale(k):
    if not WIDE:
        return np.ones(k)
    levels = np.array([30, -30])
    if k % 512:
        return np.exp2(np.random.permutation(np.resize(levels, k // 32))).repeat(32)
    a = np.empty((k // 512, 16))
    for p in range(k // 512):
        a[p, :8] = np.random.permutation(np.resize(levels, 8))
        for g in range(8):
            far = levels[np.abs(levels - a[p, g]) >= 10]
            a[p, g + 8] = far[np.random.randint(len(far))]
    return np.exp2(a.ravel()).repeat(32)


def f64(x):
    return np.asarray(x).astype(np.float64)


def striped(idx):
    return np.tile(np.asarray(idx).reshape(-1, 16).T, (8, 1)).astype(np.uint16)


def unstriped(offs):
    return offs[:16].T.reshape(-1).astype(np.int64)


E2M1 = np.array([0.0, 0.5, 1.0, 1.5, 2.0, 3.0, 4.0, 6.0, -0.0, -0.5, -1.0, -1.5, -2.0, -3.0, -4.0, -6.0])


def pack_weight(w, fmt):
    k, n = w.shape
    w = f64(np.asarray(w, np.float32).astype(ml_dtypes.bfloat16)).reshape(k // 32, 32, n)
    amax = np.abs(w).max(1)
    if fmt in ("e4m3", "e5m2"):
        byte = np.frexp(amax)[1] - 1 + 127 - (7 if fmt == "e4m3" else 14)
    else:
        mant, ex = np.frexp(amax / 6.0)
        byte = np.where(mant > 0.5, ex, ex - 1) + 127
    byte = np.clip(np.where(amax > 0, byte, 1), 1, 254)
    scaled = (w * np.exp2(127.0 - byte)[:, None, :]).reshape(k, n).astype(np.float32)
    by_word = np.ascontiguousarray(scaled.reshape(k // 512, 128, 4, n).transpose(0, 1, 3, 2))
    if fmt in ("e4m3", "e5m2"):
        words = by_word.astype(ml_dtypes.float8_e4m3fn if fmt == "e4m3" else ml_dtypes.float8_e5m2).view(np.uint8)
    else:
        c = by_word.astype(ml_dtypes.float4_e2m1fn).view(np.uint8) & 0xF
        words = (c[..., 0::2] | (c[..., 1::2] << 4)).reshape(k // 512, 128, 2 * n)
    return np.ascontiguousarray(words), np.ascontiguousarray(byte.astype(np.uint8).reshape(k // 512, 16, n))


def unpack_weight(words, scales, fmt):
    g, _, n = scales.shape
    words = np.ascontiguousarray(words).reshape(g, 128, n, -1)
    if fmt in ("e4m3", "e5m2"):
        vals = words.view(ml_dtypes.float8_e4m3fn if fmt == "e4m3" else ml_dtypes.float8_e5m2).astype(np.float64)
    else:
        nib = np.empty((g, 128, n, 4), np.uint8)
        nib[..., 0::2] = words & 0xF
        nib[..., 1::2] = words >> 4
        vals = E2M1[nib]
    vals = vals * np.repeat(np.exp2(scales.astype(np.float64) - 127.0), 8, axis=1)[..., None]
    return vals.transpose(0, 1, 3, 2).reshape(g * 512, n)


K, T, Z, J, R, C, N, E = 512, 1024, 1024, 256, 512, 512, 256, 1024


def setup_inputs():
    n = np.random.standard_normal
    idx = np.random.permutation(T)[:J]
    idx2 = np.random.permutation(Z)[:J]
    idx3 = np.random.permutation(C)[:J]
    idx4 = np.random.permutation(C)[:J]
    idx5 = np.random.permutation(E)[:J]
    fk = mx_kscale(K)
    fr = mx_kscale(R)
    xtp = pack_weight(n((K, T)) / fk[:, None], "e2m1")
    xop = pack_weight(n((K, Z)) / fk[:, None], "e5m2")
    wp = pack_weight(n((K, R)) * 1 / np.sqrt(K) * fk[:, None] * fr, "e5m2")
    wbp = pack_weight(n((R, N)) * 1 / np.sqrt(R) / fr[:, None], "e4m3")
    return {
        "xt_words": xtp[0],
        "xt_scales": xtp[1],
        "xo_words": xop[0],
        "xo_scales": xop[1],
        "w_words": wp[0],
        "w_scales": wp[1],
        "wb_words": wbp[0],
        "wb_scales": wbp[1],
        "tz": (n((N, E))).astype(np.float32),
        "offs": striped(idx),
        "offs2": striped(idx2),
        "offs3": striped(idx3),
        "offs4": striped(idx4),
        "offs5": striped(idx5),
    }


def reference(xt_words, xt_scales, xo_words, xo_scales, w_words, w_scales, wb_words, wb_scales, tz, offs, offs2, offs3, offs4, offs5):
    idx = unstriped(offs)
    idx2 = unstriped(offs2)
    idx3 = unstriped(offs3)
    idx4 = unstriped(offs4)
    idx5 = unstriped(offs5)
    xtu = unpack_weight(xt_words, xt_scales, "e2m1")
    xou = unpack_weight(xo_words, xo_scales, "e5m2")
    wu = unpack_weight(w_words, w_scales, "e5m2")
    wbu = unpack_weight(wb_words, wb_scales, "e4m3")
    xtidxg = xtu[:, idx]
    a = wu.T @ xtidxg
    xoidx2g = xou[:, idx2]
    b = wu.T @ xoidx2g
    pw = np.zeros((R, C))
    pw[:, idx3] = a
    hid = np.maximum(pw[:, idx4], b)
    hidq = mxq(hid, 0, "e5m2")
    p = wbu.T @ hidq
    y = p + f64(tz)[:, idx5]
    return y

from contextlib import ExitStack

import concourse.mybir as mybir

K, T, Z, J, R, C, N, E = 512, 1024, 1024, 256, 512, 512, 256, 1024
FLOPS = 2 * (2 * K * R * J + R * N * J)

F32 = mybir.dt.float32
BF16 = mybir.dt.bfloat16
I32 = mybir.dt.int32
U32 = mybir.dt.uint32
U16 = mybir.dt.uint16
U8 = mybir.dt.uint8
E2M1 = mybir.dt.float4_e2m1fn_x4
E5M2 = mybir.dt.float8_e5m2_x4
E4M3 = mybir.dt.float8_e4m3fn_x4
COPY = mybir.ActivationFunctionType.Copy
MAX = mybir.AluOpType.max
ADD = mybir.AluOpType.add

P = 128
PACK = 4
HALF = J // 2
LIST_COLS = J // 16


def tile_list_oneforboth_board_one_tabled_kernel(
    tc, xt_words, xt_scales, xo_words, xo_scales, w_words, w_scales, wb_words, wb_scales, tz,
    offs, offs2, offs3, offs4, offs5, out,
):
    nc = tc.nc
    with ExitStack() as ctx:
        sb = ctx.enter_context(tc.tile_pool(name="sb", bufs=1))
        ps = ctx.enter_context(tc.psum_pool(name="ps", bufs=1))

        def tile(name, shape, dtype, tag=None):
            return sb.tile(shape, dtype, name=name, tag=tag or name, align_bytes=64)

        def load_list(name, src):
            dst = tile(name, [P, LIST_COLS], U16)
            nc.sync.dma_start(dst[:], src)
            return dst

        def load_words(name, src, dtype, cols):
            dst = tile(name, [P, cols], dtype)
            nc.sync.dma_start(dst[:].bitcast(I32), src.bitcast(I32))
            return dst

        def zeroed_plane(name, cols):
            dst = tile(name, [P, cols], U8)
            nc.vector.memset(dst[:].bitcast(I32), 0)
            return dst

        def load_scale_rows(dst, src, quadrants):
            for q in quadrants:
                nc.sync.dma_start(dst[32 * q : 32 * q + 4, :].bitcast(I32), src[0, 4 * q : 4 * q + 4, :].bitcast(I32))

        def flat(words):
            return words[0].rearrange("p n t -> p (n t)")

        xt_plane = zeroed_plane("xt_plane", T)
        w_plane = zeroed_plane("w_plane", R)
        boards = [tile("board%d" % t, [P, C], F32) for t in range(PACK)]
        for t in range(PACK):
            nc.vector.memset(boards[t][:], 0.0)
        xo_plane = zeroed_plane("xo_plane", Z)
        wb_plane = zeroed_plane("wb_plane", N)

        w_raw = load_words("w_raw", flat(w_words), U32, R)
        load_scale_rows(xt_plane, xt_scales, range(4))
        token_list = load_list("token_list", offs)
        xt_raw = load_words("xt_raw", xt_words[0], U16, T)
        load_scale_rows(w_plane, w_scales, range(4))
        put_list = load_list("put_list", offs3)
        note_list = load_list("note_list", offs2)
        xo_raw = load_words("xo_raw", flat(xo_words), U32, Z)
        read_list = load_list("read_list", offs4)
        load_scale_rows(xo_plane, xo_scales, range(4))
        wb_codes = load_words("wb_codes", flat(wb_words), U32, N)
        load_scale_rows(wb_plane, wb_scales, range(4))
        entry_list = load_list("entry_list", offs5)

        w_codes = tile("w_codes", [P, R], U32)
        nc.vector.tensor_copy(w_codes[:].rearrange("p (t m) -> p m t", t=PACK), w_raw[:].rearrange("p (m t) -> p m t", t=PACK))
        xt_codes = tile("xt_codes", [P, J], U16)
        xt_scale = tile("xt_scale", [P, J], U8)
        nc.vector.tensor_copy(xt_scale[:], xt_plane[:].indirect(token_list[:]))
        nc.vector.tensor_copy(xt_codes[:], xt_raw[:].indirect(token_list[:]))
        w_scale = [tile("w_scale%d" % t, [P, P], U8) for t in range(PACK)]
        for t in range(PACK):
            nc.vector.tensor_copy(w_scale[t][:], w_plane[:, t :: PACK])

        tz_rows = []
        for u, tag in enumerate(("w_raw", "xt_raw")):
            rows = tile("tz_rows%d" % u, [P, E], F32, tag=tag)
            nc.sync.dma_start(rows[:], tz[P * u : P * (u + 1), :])
            tz_rows.append(rows)

        def w_slice(t):
            cols = slice(P * t, P * (t + 1))
            return w_codes[:, cols].bitcast(E5M2), w_scale[t][:]

        a_ps = [ps.tile([P, J], F32, name="a_ps%d" % t) for t in range(PACK)]
        for t in (0, 1, 3, 2):
            codes, scale = w_slice(t)
            nc.tensor.matmul_mx(a_ps[t][:], lhsT=codes, lhsT_scale=scale, rhs=xt_codes[:].bitcast(E2M1), rhs_scale=xt_scale[:], start=True, stop=True)

        xo_codes = tile("xo_codes", [P, J], U32)
        xo_scale = tile("xo_scale", [P, J], U8)

        a_sb = [tile("a_sb%d" % t, [P, J], F32) for t in range(PACK)]
        picked = [tile("picked0", [P, PACK, HALF], F32), tile("picked1", [P, PACK, HALF], F32, tag="xo_plane")]

        def half_of(lst, h):
            return lst[:, h * LIST_COLS // 2 : (h + 1) * LIST_COLS // 2]

        def pick_on_scalar(t, h):
            nc.scalar.activation(picked[h][:, t, :], boards[t][:].indirect(half_of(read_list, h)), COPY)

        def pick_on_vector(t, h):
            nc.vector.tensor_copy(picked[h][:, t, :], boards[t][:].indirect(half_of(read_list, h)))

        for t in (0, 1, 3):
            nc.scalar.activation(a_sb[t][:], a_ps[t][:], COPY)
        nc.scalar.activation(boards[0][:].indirect(put_list[:]), a_sb[0][:], COPY)
        nc.vector.tensor_copy(boards[1][:].indirect(put_list[:]), a_sb[1][:])
        nc.vector.tensor_copy(boards[3][:].indirect(put_list[:]), a_sb[3][:])
        nc.scalar.activation(a_sb[2][:], a_ps[2][:], COPY)
        pick_on_scalar(1, 0)
        nc.scalar.activation(boards[2][:].indirect(put_list[:]), a_sb[2][:], COPY)
        nc.vector.tensor_copy(xo_codes[:], xo_raw[:].indirect(note_list[:]))
        nc.vector.tensor_copy(xo_scale[:], xo_plane[:].indirect(note_list[:]))

        b_ps = [ps.tile([P, PACK, HALF], F32, name="b_ps%d" % h) for h in range(2)]
        for h in range(2):
            cols = slice(HALF * h, HALF * (h + 1))
            for t in range(PACK):
                codes, scale = w_slice(t)
                nc.tensor.matmul_mx(b_ps[h][:, t, :], lhsT=codes, lhsT_scale=scale, rhs=xo_codes[:, cols].bitcast(E5M2), rhs_scale=xo_scale[:, cols], start=True, stop=True)

        for t in (0, 3, 2):
            pick_on_scalar(t, 0)
        for t in (3, 1):
            pick_on_vector(t, 1)
        for t in (0, 2):
            pick_on_scalar(t, 1)

        tz_picked = [tile("tz_picked%d" % h, [P, 2, HALF], F32, tag="board%d" % (2 - 2 * h)) for h in range(2)]
        for h in range(2):
            for u in range(2):
                nc.scalar.activation(tz_picked[h][:, u, :], tz_rows[u][:].indirect(half_of(entry_list, h)), COPY)

        p_ps = [ps.tile([P, 2, HALF], F32, name="p_ps%d" % h) for h in range(2)]
        hid = [tile("hid%d" % h, [P, HALF * PACK], BF16) for h in range(2)]
        for h in range(2):
            nc.vector.tensor_tensor(
                hid[h][:].rearrange("p (c i t) -> p c t i", i=4, t=PACK),
                picked[h][:].rearrange("p t (c i) -> p c t i", i=4),
                b_ps[h][:].rearrange("p t (c i) -> p c t i", i=4),
                MAX,
            )
        for h in range(2):
            hid_codes = tile("hid_codes%d" % h, [P, HALF], U32)
            hid_scale = tile("hid_scale%d" % h, [P, HALF], U8)
            nc.vector.quantize_mx(hid_codes[:].bitcast(E5M2), hid_scale[:], hid[h][:])
            for u in range(2):
                cols = slice(P * u, P * (u + 1))
                nc.tensor.matmul_mx(p_ps[h][:, u, :], lhsT=wb_codes[:, cols].bitcast(E4M3), lhsT_scale=wb_plane[:, cols], rhs=hid_codes[:].bitcast(E5M2), rhs_scale=hid_scale[:], start=True, stop=True)

        out_rows = out.rearrange("(u p) j -> p u j", p=P)
        for h in range(2):
            y = tile("y%d" % h, [P, 2, HALF], F32)
            nc.vector.tensor_tensor(y[:], p_ps[h][:], tz_picked[h][:], ADD)
            nc.sync.dma_start(out_rows[:, :, HALF * h : HALF * (h + 1)], y[:])
